import numpy as np
import ml_dtypes


def mxq(x, axis, fmt="e4m3"):
    dtype, down = {"e4m3": (ml_dtypes.float8_e4m3fn, 7), "e5m2": (ml_dtypes.float8_e5m2, 14)}[fmt]
    v = np.moveaxis(np.asarray(x, np.float32).astype(ml_dtypes.bfloat16).astype(np.float64), axis, -1)
    blocks = v.reshape(v.shape[:-1] + (-1, 32))
    amax = np.abs(blocks).max(-1, keepdims=True)
    byte = np.maximum(np.where(amax > 0, np.frexp(amax)[1] - 1 + 127, 0) - down, 1)
    scale = np.exp2(byte - 127.0)
    codes = (blocks / scale).astype(np.float32).astype(dtype).astype(np.float64)
    return np.moveaxis((codes * scale).reshape(v.shape), -1, axis)


WIDE = False


def mx_kscale(k):
    if not WIDE:
        return np.ones(k)
    levels = np.array([10, -10, 5, -5, 0])
    if k % 512:
        return np.exp2(np.random.permutation(np.resize(levels, k // 32))).repeat(32)
    a = np.empty((k // 512, 16))
    for p in range(k // 512):
        a[p, :8] = np.random.permutation(np.resize(levels, 8))
        for g in range(8):
            far = levels[np.abs(levels - a[p, g]) >= 10]
            a[p, g + 8] = far[np.random.randint(len(far))]
    return np.exp2(a.ravel()).repeat(32)


def f64(x):
    return np.asarray(x).astype(np.float64)


def striped(idx):
    return np.tile(idx.reshape(-1, 16).T, (8, 1)).astype(np.uint16)


def unstriped(offs):
    return offs[:16].T.reshape(-1).astype(np.int64)


def pack_weight(w):
    k, n = w.shape
    w = f64(np.asarray(w, np.float32).astype(ml_dtypes.bfloat16)).reshape(k // 32, 32, n)
    amax = np.abs(w).max(1)
    byte = np.clip(np.where(amax > 0, np.frexp(amax)[1] - 1 + 127 - 7, 1), 1, 254)
    scaled = (w * np.exp2(127.0 - byte)[:, None, :]).reshape(k, n).astype(np.float32)
    words = np.ascontiguousarray(scaled.reshape(k // 512, 128, 4, n).transpose(0, 1, 3, 2)).astype(ml_dtypes.float8_e4m3fn).view(np.uint8)
    return words, np.ascontiguousarray(byte.astype(np.uint8).reshape(k // 512, 16, n))


def unpack_weight(words, scales):
    g, p, n, _ = words.shape
    vals = np.ascontiguousarray(words).view(ml_dtypes.float8_e4m3fn).astype(np.float64) * np.repeat(np.exp2(scales.astype(np.float64) - 127.0), 8, axis=1)[..., None]
    return vals.transpose(0, 1, 3, 2).reshape(g * 512, n)


K, T, S, N, U, V = 1024, 2048, 512, 128, 512, 256
P = 2 ** 7


def setup_inputs():
    n = np.random.standard_normal
    s = mx_kscale(K)[:, None]
    packed_xT = pack_weight(n((K, T)) * s)
    return {
        "x_words": packed_xT[0],
        "x_scales": packed_xT[1],
        "w1": (n((K, N)) / np.sqrt(K) / s).astype(np.float32),
        "w2": (n((K, N)) / np.sqrt(K) / s).astype(np.float32),
        "state": (n((N, V))).astype(np.float32),
        "dtv": (np.tile(np.random.uniform(0.1, 0.5, V), (P, 1))).astype(np.float32),
        "offs": striped(np.random.permutation(T)[:S]),
        "lc": striped(np.random.randint(0, S, U)),
        "rc": striped(np.random.randint(0, S, U)),
        "outf": striped(np.random.permutation(U)[:V]),
        "inf": striped(np.random.permutation(U)[:V]),
    }


def reference(x_words, x_scales, w1, w2, state, dtv, offs, lc, rc, outf, inf):
    xq = unpack_weight(x_words, x_scales)[:, unstriped(offs)]
    y = mxq(f64(w1), 0, "e4m3").T @ xq
    ul = y[:, unstriped(lc)]
    z = mxq(f64(w2), 0, "e4m3").T @ xq
    snd = np.log(np.exp(z) + 1.0) + 0.3
    al = snd[:, unstriped(lc)]
    ur = y[:, unstriped(rc)]
    ar = snd[:, unstriped(rc)]
    sr = np.maximum(np.maximum(ul + al, ur + ar), 0.01 * ar)
    sl = np.minimum(np.minimum(ul - al, ur - ar), -0.01 * al)
    wd = sr - sl
    flux = (0.5 * (sr * ((ul) ** 2) - (sl * ((ur) ** 2))) + (sl * sr) * (ur - ul)) / wd
    return f64(state) - ((flux[:, unstriped(outf)] - flux[:, unstriped(inf)]) * f64(dtv)[:1])

@@ -1,0 +1,166 @@
+import math
+from contextlib import ExitStack
+
+import concourse.mybir as mybir
+
+K, T, S, N, U, V = 1024, 2048, 512, 128, 512, 256
+FLOPS = 2 * 2 * K * N * S
+
+F32 = mybir.dt.float32
+BF16 = mybir.dt.bfloat16
+I32 = mybir.dt.int32
+U32 = mybir.dt.uint32
+U16 = mybir.dt.uint16
+U8 = mybir.dt.uint8
+FP8X4 = mybir.dt.float8_e4m3fn_x4
+ACT = mybir.ActivationFunctionType
+ALU = mybir.AluOpType
+
+P = 128
+PACK = 4
+PASSES = K // (P * PACK)
+HALF = S // 2
+WINDOW = 704
+LIST_ROWS = 16
+
+
+def tile_picked_yhllf_step_p_kernel(
+    tc, x_words, x_scales, w1, w2, state, dtv, offs, lc, rc, outf, inf, out
+):
+    nc = tc.nc
+    with ExitStack() as ctx:
+        lists = ctx.enter_context(tc.tile_pool(name="lists", bufs=1))
+        sb = ctx.enter_context(tc.tile_pool(name="sb", bufs=1))
+        psum = ctx.enter_context(tc.psum_pool(name="psum", bufs=1))
+
+        def f32(name, width=U):
+            return sb.tile([P, width], F32, name=name)
+
+        def load_list(name, src):
+            t = lists.tile(list(src.shape), U16, name=name)
+            nc.sync.dma_start(t[:], src)
+            return t
+
+        offs_t = load_list("offs_t", offs)
+
+        table_scales = sb.tile([P, T], U8, name="table_scales")
+        nc.vector.memset(table_scales[:].bitcast(I32), 0)
+        for q in range(4):
+            nc.scalar.dma_start(
+                table_scales[32 * q : 32 * q + 4 * PASSES, :].bitcast(I32),
+                x_scales[:, 4 * q : 4 * q + 4, :].bitcast(I32),
+            )
+
+        w_raw = []
+        for name, w in (("w1", w1), ("w2", w2)):
+            raw = sb.tile([P, PASSES, PACK, N], F32, name=name + "_raw")
+            nc.sync.dma_start(raw[:], w.rearrange("(g p j) n -> p g j n", g=PASSES, j=PACK))
+            w_raw.append(raw)
+        table_words = []
+        for g in range(PASSES):
+            words = sb.tile([P, T], U32, name="table_words%d" % g)
+            nc.sync.dma_start(words[:].bitcast(I32), x_words[g].rearrange("p n t -> p (n t)").bitcast(I32))
+            table_words.append(words)
+        lc_t = load_list("lc_t", lc)
+        rc_t = load_list("rc_t", rc)
+        outf_t = load_list("outf_t", outf)
+        inf_t = load_list("inf_t", inf)
+        state_t = f32("state_t", V)
+        dt_t = f32("dt_t", V)
+        nc.sync.dma_start(state_t[:], state)
+        nc.sync.dma_start(dt_t[:], dtv)
+
+        y = f32("y", WINDOW)
+        snd = f32("snd", WINDOW)
+        nc.gpsimd.memset(y[:, S:], 0.0)
+        nc.gpsimd.memset(snd[:, S:], 0.0)
+
+        w_codes, w_scales = [], []
+        for i, raw in enumerate(w_raw):
+            grouped = sb.tile([P, PASSES, N, PACK], BF16, name="grouped%d" % i, align_bytes=64)
+            nc.scalar.copy(out=grouped[:], in_=raw[:].rearrange("p g j n -> p g n j"))
+            codes = sb.tile([P, PASSES * N], U32, name="w_codes%d" % i, align_bytes=64)
+            scales = sb.tile([P, PASSES * N], U8, name="w_scales%d" % i, align_bytes=64)
+            nc.vector.quantize_mx(
+                out=codes[:].bitcast(FP8X4), scales=scales[:], in_=grouped[:].rearrange("p g n j -> p (g n j)")
+            )
+            w_codes.append(codes)
+            w_scales.append(scales)
+
+        picked_scales = sb.tile([P, S], U8, name="picked_scales", align_bytes=64)
+        nc.vector.tensor_copy(picked_scales[:], table_scales[:].indirect(offs_t[:]))
+
+        halves = [slice(h * HALF, (h + 1) * HALF) for h in range(2)]
+        acc = [[psum.tile([P, HALF], F32, name="acc%d%d" % (i, h)) for h in range(2)] for i in range(2)]
+        for g in range(PASSES):
+            for h, cols in enumerate(halves):
+                picked = sb.tile([P, HALF], U32, name="picked%d%d" % (g, h), align_bytes=64)
+                entries = offs_t[:, cols.start // LIST_ROWS : cols.stop // LIST_ROWS]
+                nc.vector.tensor_copy(picked[:], table_words[g][:].indirect(entries))
+                for i in range(2):
+                    nc.tensor.matmul_mx(
+                        out=acc[i][h][:],
+                        lhsT=w_codes[i][:, g * N : (g + 1) * N].bitcast(FP8X4),
+                        lhsT_scale=w_scales[i][:, g * N : (g + 1) * N],
+                        rhs=picked[:].bitcast(FP8X4),
+                        rhs_scale=picked_scales[4 * g :, cols],
+                        start=(g == 0),
+                        stop=(g == PASSES - 1),
+                    )
+        y_acc, z_acc = acc
+
+        z_abs, z_exp, z_log = f32("z_abs"), f32("z_exp"), f32("z_log")
+        for h, cols in enumerate(halves):
+            nc.vector.tensor_copy(y[:, cols], y_acc[h][:])
+            nc.scalar.activation(z_abs[:, cols], z_acc[h][:], ACT.Abs)
+            nc.scalar.activation(z_exp[:, cols], z_abs[:, cols], ACT.Exp, scale=-1.0)
+        shift = math.exp(0.3)
+        nc.scalar.activation(z_log[:], z_exp[:], ACT.Ln, scale=shift, bias=shift)
+
+        ul, ur, al, ar = f32("ul"), f32("ur"), f32("al"), f32("ar")
+        nc.vector.tensor_copy(ul[:], y[:].indirect(lc_t[:]))
+        nc.vector.tensor_copy(ur[:], y[:].indirect(rc_t[:]))
+        half_sq = f32("half_sq")
+        nc.scalar.activation(half_sq[:], ul[:], ACT.Square, scale=math.sqrt(0.5))
+        jump, total = f32("jump"), f32("total")
+        nc.vector.tensor_tensor(jump[:], ur[:], ul[:], ALU.subtract)
+        for h, cols in enumerate(halves):
+            nc.vector.scalar_tensor_tensor(snd[:, cols], z_acc[h][:], 0.0, z_log[:, cols], ALU.max, ALU.add)
+        nc.vector.tensor_tensor(total[:], ur[:], ul[:], ALU.add)
+        nc.vector.tensor_copy(al[:], snd[:].indirect(lc_t[:]))
+        nc.vector.tensor_copy(ar[:], snd[:].indirect(rc_t[:]))
+
+        back_l, back_r, fwd_l, fwd_r = f32("back_l"), f32("back_r"), f32("fwd_l"), f32("fwd_r")
+        floor_b, floor_f, back, fwd = f32("floor_b"), f32("floor_f"), f32("back"), f32("fwd")
+        nc.vector.tensor_tensor(back_l[:], al[:], ul[:], ALU.subtract)
+        nc.vector.tensor_tensor(fwd_l[:], al[:], ul[:], ALU.add)
+        nc.vector.tensor_tensor(fwd_r[:], ar[:], ur[:], ALU.add)
+        nc.vector.scalar_tensor_tensor(floor_b[:], al[:], 0.01, back_l[:], ALU.mult, ALU.max)
+        nc.vector.tensor_tensor(back_r[:], ar[:], ur[:], ALU.subtract)
+        nc.vector.scalar_tensor_tensor(floor_f[:], ar[:], 0.01, fwd_r[:], ALU.mult, ALU.max)
+        nc.vector.tensor_tensor(back[:], floor_b[:], back_r[:], ALU.max)
+        nc.vector.tensor_tensor(fwd[:], floor_f[:], fwd_l[:], ALU.max)
+
+        jump_back, width, root, inv = f32("jump_back"), f32("width"), f32("root"), f32("inv")
+        lag, numer, corr, flux = f32("lag"), f32("numer"), f32("corr"), f32("flux")
+        nc.vector.tensor_tensor(jump_back[:], jump[:], back[:], ALU.mult)
+        for cols in halves:
+            nc.vector.tensor_tensor(width[:, cols], fwd[:, cols], back[:, cols], ALU.add)
+        for cols in halves:
+            nc.scalar.activation(root[:, cols], width[:, cols], ACT.Abs_reciprocal_sqrt)
+        for cols in halves:
+            nc.scalar.activation(inv[:, cols], root[:, cols], ACT.Square)
+        nc.vector.scalar_tensor_tensor(lag[:], total[:], 0.5, fwd[:], ALU.mult, ALU.subtract)
+        for cols in halves:
+            nc.vector.tensor_tensor(numer[:, cols], lag[:, cols], jump_back[:, cols], ALU.mult)
+        for cols in halves:
+            nc.vector.tensor_tensor(corr[:, cols], numer[:, cols], inv[:, cols], ALU.mult)
+        for cols in halves:
+            nc.vector.tensor_tensor(flux[:, cols], corr[:, cols], half_sq[:, cols], ALU.add)
+
+        gain, loss, part, new = f32("gain", V), f32("loss", V), f32("part", V), f32("new", V)
+        nc.vector.tensor_tensor(gain[:], flux[:].indirect(inf_t[:]), dt_t[:], ALU.mult)
+        nc.vector.tensor_tensor(loss[:], flux[:].indirect(outf_t[:]), dt_t[:], ALU.mult)
+        nc.vector.tensor_tensor(part[:], gain[:], state_t[:], ALU.add)
+        nc.vector.tensor_tensor(new[:], part[:], loss[:], ALU.subtract)
+        nc.sync.dma_start(out, new[:])

@@ -22,6 +22,7 @@ PASSES = K // (P * PACK)
 HALF = S // 2
 WINDOW = 704
 LIST_ROWS = 16
+TINY = 2.0**-63
 
 
 def tile_picked_yhllf_step_p_kernel(
@@ -72,13 +73,16 @@ def tile_picked_yhllf_step_p_kernel(
 
         y = f32("y", WINDOW)
         snd = f32("snd", WINDOW)
-        nc.gpsimd.memset(y[:, S:], 0.0)
-        nc.gpsimd.memset(snd[:, S:], 0.0)
+        nc.vector.memset(y[:, S:], 0.0)
+        nc.vector.memset(snd[:, S:], 0.0)
+
+        warm = f32("warm", 8)
+        nc.scalar.activation(warm[:], y[:, S : S + 8], ACT.Sigmoid)
 
         w_codes, w_scales = [], []
         for i, raw in enumerate(w_raw):
             grouped = sb.tile([P, PASSES, N, PACK], BF16, name="grouped%d" % i, align_bytes=64)
-            nc.scalar.copy(out=grouped[:], in_=raw[:].rearrange("p g j n -> p g n j"))
+            nc.scalar.activation(grouped[:], raw[:].rearrange("p g j n -> p g n j"), ACT.Copy, scale=(1.0, -1.0)[i])
             codes = sb.tile([P, PASSES * N], U32, name="w_codes%d" % i, align_bytes=64)
             scales = sb.tile([P, PASSES * N], U8, name="w_scales%d" % i, align_bytes=64)
             nc.vector.quantize_mx(
@@ -109,58 +113,65 @@ def tile_picked_yhllf_step_p_kernel(
                     )
         y_acc, z_acc = acc
 
-        z_abs, z_exp, z_log = f32("z_abs"), f32("z_exp"), f32("z_log")
+        sig, log_sig = f32("sig"), f32("log_sig")
         for h, cols in enumerate(halves):
             nc.vector.tensor_copy(y[:, cols], y_acc[h][:])
-            nc.scalar.activation(z_abs[:, cols], z_acc[h][:], ACT.Abs)
-            nc.scalar.activation(z_exp[:, cols], z_abs[:, cols], ACT.Exp, scale=-1.0)
-        shift = math.exp(0.3)
-        nc.scalar.activation(z_log[:], z_exp[:], ACT.Ln, scale=shift, bias=shift)
+            nc.scalar.activation(sig[:, cols], z_acc[h][:], ACT.Sigmoid)
+        shrink = math.exp(-0.3)
+        nc.scalar.activation(log_sig[:], sig[:], ACT.Ln, scale=shrink, bias=shrink * TINY)
 
-        ul, ur, al, ar = f32("ul"), f32("ur"), f32("al"), f32("ar")
+        ul, ur, nl, nr = f32("ul"), f32("ur"), f32("nl"), f32("nr")
         nc.vector.tensor_copy(ul[:], y[:].indirect(lc_t[:]))
         nc.vector.tensor_copy(ur[:], y[:].indirect(rc_t[:]))
         half_sq = f32("half_sq")
         nc.scalar.activation(half_sq[:], ul[:], ACT.Square, scale=math.sqrt(0.5))
         jump, total = f32("jump"), f32("total")
-        nc.vector.tensor_tensor(jump[:], ur[:], ul[:], ALU.subtract)
         for h, cols in enumerate(halves):
-            nc.vector.scalar_tensor_tensor(snd[:, cols], z_acc[h][:], 0.0, z_log[:, cols], ALU.max, ALU.add)
-        nc.vector.tensor_tensor(total[:], ur[:], ul[:], ALU.add)
-        nc.vector.tensor_copy(al[:], snd[:].indirect(lc_t[:]))
-        nc.vector.tensor_copy(ar[:], snd[:].indirect(rc_t[:]))
+            nc.vector.scalar_tensor_tensor(snd[:, cols], z_acc[h][:], -0.3, log_sig[:, cols], ALU.add, ALU.min)
+        nc.vector.tensor_tensor(jump[:], ur[:], ul[:], ALU.subtract)
+        nc.vector.tensor_copy(nl[:], snd[:].indirect(lc_t[:]))
+        nc.vector.tensor_copy(nr[:], snd[:].indirect(rc_t[:]))
 
         back_l, back_r, fwd_l, fwd_r = f32("back_l"), f32("back_r"), f32("fwd_l"), f32("fwd_r")
-        floor_b, floor_f, back, fwd = f32("floor_b"), f32("floor_f"), f32("back"), f32("fwd")
-        nc.vector.tensor_tensor(back_l[:], al[:], ul[:], ALU.subtract)
-        nc.vector.tensor_tensor(fwd_l[:], al[:], ul[:], ALU.add)
-        nc.vector.tensor_tensor(fwd_r[:], ar[:], ur[:], ALU.add)
-        nc.vector.scalar_tensor_tensor(floor_b[:], al[:], 0.01, back_l[:], ALU.mult, ALU.max)
-        nc.vector.tensor_tensor(back_r[:], ar[:], ur[:], ALU.subtract)
-        nc.vector.scalar_tensor_tensor(floor_f[:], ar[:], 0.01, fwd_r[:], ALU.mult, ALU.max)
-        nc.vector.tensor_tensor(back[:], floor_b[:], back_r[:], ALU.max)
-        nc.vector.tensor_tensor(fwd[:], floor_f[:], fwd_l[:], ALU.max)
+        cap_l, cap_r, sl, sr = f32("cap_l"), f32("cap_r"), f32("sl"), f32("sr")
+        nc.vector.tensor_tensor(back_l[:], ul[:], nl[:], ALU.add)
+        nc.vector.tensor_tensor(fwd_l[:], ul[:], nl[:], ALU.subtract)
+        nc.vector.tensor_tensor(fwd_r[:], ur[:], nr[:], ALU.subtract)
+        nc.vector.scalar_tensor_tensor(cap_l[:], nl[:], 0.01, back_l[:], ALU.mult, ALU.min)
+        nc.vector.tensor_tensor(back_r[:], ur[:], nr[:], ALU.add)
+        nc.vector.scalar_tensor_tensor(cap_r[:], nr[:], -0.01, fwd_r[:], ALU.mult, ALU.max)
+        nc.vector.tensor_tensor(sl[:], cap_l[:], back_r[:], ALU.min)
+        nc.vector.tensor_tensor(sr[:], cap_r[:], fwd_l[:], ALU.max)
 
-        jump_back, width, root, inv = f32("jump_back"), f32("width"), f32("root"), f32("inv")
-        lag, numer, corr, flux = f32("lag"), f32("numer"), f32("corr"), f32("flux")
-        nc.vector.tensor_tensor(jump_back[:], jump[:], back[:], ALU.mult)
+        jump_sl, width, root, inv = f32("jump_sl"), f32("width"), f32("root"), f32("inv")
+        lead, numer, corr, flux = f32("lead"), f32("numer"), f32("corr"), f32("flux")
+        nc.vector.tensor_tensor(total[:], ur[:], ul[:], ALU.add)
         for cols in halves:
-            nc.vector.tensor_tensor(width[:, cols], fwd[:, cols], back[:, cols], ALU.add)
+            nc.vector.tensor_tensor(width[:, cols], sr[:, cols], sl[:, cols], ALU.subtract)
         for cols in halves:
             nc.scalar.activation(root[:, cols], width[:, cols], ACT.Abs_reciprocal_sqrt)
         for cols in halves:
             nc.scalar.activation(inv[:, cols], root[:, cols], ACT.Square)
-        nc.vector.scalar_tensor_tensor(lag[:], total[:], 0.5, fwd[:], ALU.mult, ALU.subtract)
+        nc.vector.tensor_tensor(jump_sl[:], jump[:], sl[:], ALU.mult)
+        nc.vector.scalar_tensor_tensor(lead[:], total[:], -0.5, sr[:], ALU.mult, ALU.add)
         for cols in halves:
-            nc.vector.tensor_tensor(numer[:, cols], lag[:, cols], jump_back[:, cols], ALU.mult)
+            nc.vector.tensor_tensor(numer[:, cols], lead[:, cols], jump_sl[:, cols], ALU.mult)
         for cols in halves:
             nc.vector.tensor_tensor(corr[:, cols], numer[:, cols], inv[:, cols], ALU.mult)
         for cols in halves:
             nc.vector.tensor_tensor(flux[:, cols], corr[:, cols], half_sq[:, cols], ALU.add)
 
         gain, loss, part, new = f32("gain", V), f32("loss", V), f32("part", V), f32("new", V)
+        cells = [slice(h * V // 2, (h + 1) * V // 2) for h in range(2)]
+
+        def outflow(cols):
+            entries = outf_t[:, cols.start // LIST_ROWS : cols.stop // LIST_ROWS]
+            nc.vector.tensor_tensor(loss[:, cols], flux[:].indirect(entries), dt_t[:, cols], ALU.mult)
+
         nc.vector.tensor_tensor(gain[:], flux[:].indirect(inf_t[:]), dt_t[:], ALU.mult)
-        nc.vector.tensor_tensor(loss[:], flux[:].indirect(outf_t[:]), dt_t[:], ALU.mult)
+        outflow(cells[0])
         nc.vector.tensor_tensor(part[:], gain[:], state_t[:], ALU.add)
-        nc.vector.tensor_tensor(new[:], part[:], loss[:], ALU.subtract)
-        nc.sync.dma_start(out, new[:])
+        outflow(cells[1])
+        for cols in cells:
+            nc.vector.tensor_tensor(new[:, cols], part[:, cols], loss[:, cols], ALU.subtract)
+            nc.sync.dma_start(out[:, cols], new[:, cols])

@@ -128,7 +128,8 @@ def tile_picked_yhllf_step_p_kernel(
         jump, total = f32("jump"), f32("total")
         for h, cols in enumerate(halves):
             nc.vector.scalar_tensor_tensor(snd[:, cols], z_acc[h][:], -0.3, log_sig[:, cols], ALU.add, ALU.min)
-        nc.vector.tensor_tensor(jump[:], ur[:], ul[:], ALU.subtract)
+        nc.gpsimd.tensor_tensor(jump[:], ur[:], ul[:], ALU.subtract)
+        nc.gpsimd.tensor_tensor(total[:], ur[:], ul[:], ALU.add)
         nc.vector.tensor_copy(nl[:], snd[:].indirect(lc_t[:]))
         nc.vector.tensor_copy(nr[:], snd[:].indirect(rc_t[:]))
 
@@ -141,11 +142,11 @@ def tile_picked_yhllf_step_p_kernel(
         nc.vector.tensor_tensor(back_r[:], ur[:], nr[:], ALU.add)
         nc.vector.scalar_tensor_tensor(cap_r[:], nr[:], -0.01, fwd_r[:], ALU.mult, ALU.max)
         nc.vector.tensor_tensor(sl[:], cap_l[:], back_r[:], ALU.min)
-        nc.vector.tensor_tensor(sr[:], cap_r[:], fwd_l[:], ALU.max)
+        for cols in halves:
+            nc.vector.tensor_tensor(sr[:, cols], cap_r[:, cols], fwd_l[:, cols], ALU.max)
 
         jump_sl, width, root, inv = f32("jump_sl"), f32("width"), f32("root"), f32("inv")
         lead, numer, corr, flux = f32("lead"), f32("numer"), f32("corr"), f32("flux")
-        nc.vector.tensor_tensor(total[:], ur[:], ul[:], ALU.add)
         for cols in halves:
             nc.vector.tensor_tensor(width[:, cols], sr[:, cols], sl[:, cols], ALU.subtract)
         for cols in halves:

@@ -42,8 +42,6 @@ def tile_picked_yhllf_step_p_kernel(
             nc.sync.dma_start(t[:], src)
             return t
 
-        offs_t = load_list("offs_t", offs)
-
         table_scales = sb.tile([P, T], U8, name="table_scales")
         nc.vector.memset(table_scales[:].bitcast(I32), 0)
         for q in range(4):
@@ -57,6 +55,7 @@ def tile_picked_yhllf_step_p_kernel(
             raw = sb.tile([P, PASSES, PACK, N], F32, name=name + "_raw")
             nc.sync.dma_start(raw[:], w.rearrange("(g p j) n -> p g j n", g=PASSES, j=PACK))
             w_raw.append(raw)
+        offs_t = load_list("offs_t", offs)
         table_words = []
         for g in range(PASSES):
             words = sb.tile([P, T], U32, name="table_words%d" % g)
@@ -81,8 +80,9 @@ def tile_picked_yhllf_step_p_kernel(
 
         w_codes, w_scales = [], []
         for i, raw in enumerate(w_raw):
-            grouped = sb.tile([P, PASSES, N, PACK], BF16, name="grouped%d" % i, align_bytes=64)
-            nc.scalar.activation(grouped[:], raw[:].rearrange("p g j n -> p g n j"), ACT.Copy, scale=(1.0, -1.0)[i])
+            grouped = sb.tile([P, PASSES, N, PACK], BF16, name="grouped", tag="grouped%d" % i, align_bytes=64)
+            side_by_side = raw[:].rearrange("p g j n -> p g n j")
+            nc.vector.tensor_scalar(grouped[:], side_by_side, (1.0, -1.0)[i], None, ALU.mult)
             codes = sb.tile([P, PASSES * N], U32, name="w_codes%d" % i, align_bytes=64)
             scales = sb.tile([P, PASSES * N], U8, name="w_scales%d" % i, align_bytes=64)
             nc.vector.quantize_mx(
@@ -91,7 +91,7 @@ def tile_picked_yhllf_step_p_kernel(
             w_codes.append(codes)
             w_scales.append(scales)
 
-        picked_scales = sb.tile([P, S], U8, name="picked_scales", align_bytes=64)
+        picked_scales = sb.tile([P, S], U8, name="picked_scales", tag="grouped1", align_bytes=64)
         nc.vector.tensor_copy(picked_scales[:], table_scales[:].indirect(offs_t[:]))
 
         halves = [slice(h * HALF, (h + 1) * HALF) for h in range(2)]
@@ -115,10 +115,11 @@ def tile_picked_yhllf_step_p_kernel(
 
         sig, log_sig = f32("sig"), f32("log_sig")
         for h, cols in enumerate(halves):
-            nc.vector.tensor_copy(y[:, cols], y_acc[h][:])
+            nc.scalar.copy(y[:, cols], y_acc[h][:])
             nc.scalar.activation(sig[:, cols], z_acc[h][:], ACT.Sigmoid)
         shrink = math.exp(-0.3)
-        nc.scalar.activation(log_sig[:], sig[:], ACT.Ln, scale=shrink, bias=shrink * TINY)
+        for cols in halves:
+            nc.scalar.activation(log_sig[:, cols], sig[:, cols], ACT.Ln, scale=shrink, bias=shrink * TINY)
 
         ul, ur, nl, nr = f32("ul"), f32("ur"), f32("nl"), f32("nr")
         nc.vector.tensor_copy(ul[:], y[:].indirect(lc_t[:]))
@@ -136,7 +137,8 @@ def tile_picked_yhllf_step_p_kernel(
         back_l, back_r, fwd_l, fwd_r = f32("back_l"), f32("back_r"), f32("fwd_l"), f32("fwd_r")
         cap_l, cap_r, sl, sr = f32("cap_l"), f32("cap_r"), f32("sl"), f32("sr")
         nc.vector.tensor_tensor(back_l[:], ul[:], nl[:], ALU.add)
-        nc.vector.tensor_tensor(fwd_l[:], ul[:], nl[:], ALU.subtract)
+        for engine, cols in zip((nc.gpsimd, nc.vector), halves):
+            engine.tensor_tensor(fwd_l[:, cols], ul[:, cols], nl[:, cols], ALU.subtract)
         nc.vector.tensor_tensor(fwd_r[:], ur[:], nr[:], ALU.subtract)
         nc.vector.scalar_tensor_tensor(cap_l[:], nl[:], 0.01, back_l[:], ALU.mult, ALU.min)
         nc.vector.tensor_tensor(back_r[:], ur[:], nr[:], ALU.add)

@@ -19,10 +19,17 @@ ALU = mybir.AluOpType
 P = 128
 PACK = 4
 PASSES = K // (P * PACK)
-HALF = S // 2
-WINDOW = 704
+QUADRANT = 32
+SCALE_ROWS = 4
 LIST_ROWS = 16
+MX_ALIGN = 64
+SPEED_FLOOR = 0.3
+CLAMP = 0.01
 TINY = 2.0**-63
+
+
+def halves_of(width):
+    return [slice(0, width // 2), slice(width // 2, width)]
 
 
 def tile_picked_yhllf_step_p_kernel(
@@ -34,32 +41,35 @@ def tile_picked_yhllf_step_p_kernel(
         sb = ctx.enter_context(tc.tile_pool(name="sb", bufs=1))
         psum = ctx.enter_context(tc.psum_pool(name="psum", bufs=1))
 
-        def f32(name, width=U):
+        def f32(name, width):
             return sb.tile([P, width], F32, name=name)
 
+        def looked_up(window, offsets, cols):
+            return window[:].indirect(offsets[:, cols.start // LIST_ROWS : cols.stop // LIST_ROWS])
+
         def load_list(name, src):
-            t = lists.tile(list(src.shape), U16, name=name)
-            nc.sync.dma_start(t[:], src)
-            return t
+            offsets = lists.tile(list(src.shape), U16, name=name)
+            nc.sync.dma_start(offsets[:], src)
+            return offsets
 
         table_scales = sb.tile([P, T], U8, name="table_scales")
         nc.vector.memset(table_scales[:].bitcast(I32), 0)
-        for q in range(4):
+        for q in range(P // QUADRANT):
             nc.scalar.dma_start(
-                table_scales[32 * q : 32 * q + 4 * PASSES, :].bitcast(I32),
-                x_scales[:, 4 * q : 4 * q + 4, :].bitcast(I32),
+                table_scales[QUADRANT * q : QUADRANT * q + SCALE_ROWS * PASSES, :].bitcast(I32),
+                x_scales[:, SCALE_ROWS * q : SCALE_ROWS * (q + 1), :].bitcast(I32),
             )
 
         w_raw = []
-        for name, w in (("w1", w1), ("w2", w2)):
-            raw = sb.tile([P, PASSES, PACK, N], F32, name=name + "_raw")
-            nc.sync.dma_start(raw[:], w.rearrange("(g p j) n -> p g j n", g=PASSES, j=PACK))
+        for name, w in (("w1_raw", w1), ("w2_raw", w2)):
+            raw = sb.tile([P, PASSES, PACK, N], F32, name=name)
+            nc.sync.dma_start(raw[:], w.rearrange("(g p t) m -> p g t m", g=PASSES, t=PACK))
             w_raw.append(raw)
         offs_t = load_list("offs_t", offs)
         table_words = []
         for g in range(PASSES):
             words = sb.tile([P, T], U32, name="table_words%d" % g)
-            nc.sync.dma_start(words[:].bitcast(I32), x_words[g].rearrange("p n t -> p (n t)").bitcast(I32))
+            nc.sync.dma_start(words[:].bitcast(I32), x_words[g].rearrange("p c t -> p (c t)").bitcast(I32))
             table_words.append(words)
         lc_t = load_list("lc_t", lc)
         rc_t = load_list("rc_t", rc)
@@ -70,111 +80,114 @@ def tile_picked_yhllf_step_p_kernel(
         nc.sync.dma_start(state_t[:], state)
         nc.sync.dma_start(dt_t[:], dtv)
 
-        y = f32("y", WINDOW)
-        snd = f32("snd", WINDOW)
-        nc.vector.memset(y[:, S:], 0.0)
-        nc.vector.memset(snd[:, S:], 0.0)
-
-        warm = f32("warm", 8)
-        nc.scalar.activation(warm[:], y[:, S : S + 8], ACT.Sigmoid)
+        warm_in, warm_out = f32("warm_in", 8), f32("warm_out", 8)
+        nc.vector.memset(warm_in[:], 0.0)
+        nc.scalar.activation(warm_out[:], warm_in[:], ACT.Sigmoid)
 
         w_codes, w_scales = [], []
-        for i, raw in enumerate(w_raw):
-            grouped = sb.tile([P, PASSES, N, PACK], BF16, name="grouped", tag="grouped%d" % i, align_bytes=64)
-            side_by_side = raw[:].rearrange("p g j n -> p g n j")
-            nc.vector.tensor_scalar(grouped[:], side_by_side, (1.0, -1.0)[i], None, ALU.mult)
-            codes = sb.tile([P, PASSES * N], U32, name="w_codes%d" % i, align_bytes=64)
-            scales = sb.tile([P, PASSES * N], U8, name="w_scales%d" % i, align_bytes=64)
+        for i, (raw, sign) in enumerate(zip(w_raw, (1.0, -1.0))):
+            grouped = sb.tile([P, PASSES, N, PACK], BF16, name="grouped", tag="grouped%d" % i, align_bytes=MX_ALIGN)
+            nc.vector.tensor_scalar(grouped[:], raw[:].rearrange("p g t m -> p g m t"), sign, None, ALU.mult)
+            codes = sb.tile([P, PASSES * N], U32, name="w_codes%d" % i, align_bytes=MX_ALIGN)
+            scales = sb.tile([P, PASSES * N], U8, name="w_scales%d" % i, align_bytes=MX_ALIGN)
             nc.vector.quantize_mx(
-                out=codes[:].bitcast(FP8X4), scales=scales[:], in_=grouped[:].rearrange("p g n j -> p (g n j)")
+                out=codes[:].bitcast(FP8X4), scales=scales[:], in_=grouped[:].rearrange("p g m t -> p (g m t)")
             )
             w_codes.append(codes)
             w_scales.append(scales)
 
-        picked_scales = sb.tile([P, S], U8, name="picked_scales", tag="grouped1", align_bytes=64)
+        picked_scales = sb.tile([P, S], U8, name="picked_scales", tag="grouped1", align_bytes=MX_ALIGN)
         nc.vector.tensor_copy(picked_scales[:], table_scales[:].indirect(offs_t[:]))
 
-        halves = [slice(h * HALF, (h + 1) * HALF) for h in range(2)]
-        acc = [[psum.tile([P, HALF], F32, name="acc%d%d" % (i, h)) for h in range(2)] for i in range(2)]
+        cell_halves = halves_of(S)
+        acc = [[psum.tile([P, S // 2], F32, name="acc%d%d" % (i, h)) for h in range(2)] for i in range(2)]
         for g in range(PASSES):
-            for h, cols in enumerate(halves):
-                picked = sb.tile([P, HALF], U32, name="picked%d%d" % (g, h), align_bytes=64)
-                entries = offs_t[:, cols.start // LIST_ROWS : cols.stop // LIST_ROWS]
-                nc.vector.tensor_copy(picked[:], table_words[g][:].indirect(entries))
+            for h, cols in enumerate(cell_halves):
+                picked = sb.tile([P, S // 2], U32, name="picked%d%d" % (g, h), align_bytes=MX_ALIGN)
+                nc.vector.tensor_copy(picked[:], looked_up(table_words[g], offs_t, cols))
                 for i in range(2):
                     nc.tensor.matmul_mx(
                         out=acc[i][h][:],
                         lhsT=w_codes[i][:, g * N : (g + 1) * N].bitcast(FP8X4),
                         lhsT_scale=w_scales[i][:, g * N : (g + 1) * N],
                         rhs=picked[:].bitcast(FP8X4),
-                        rhs_scale=picked_scales[4 * g :, cols],
+                        rhs_scale=picked_scales[SCALE_ROWS * g :, cols],
                         start=(g == 0),
                         stop=(g == PASSES - 1),
                     )
-        y_acc, z_acc = acc
+        y_acc, neg_z_acc = acc
 
-        sig, log_sig = f32("sig"), f32("log_sig")
-        for h, cols in enumerate(halves):
+        y, neg_snd = f32("y", S), f32("neg_snd", S)
+        sig, log_sig = f32("sig", S), f32("log_sig", S)
+        for h, cols in enumerate(cell_halves):
             nc.scalar.copy(y[:, cols], y_acc[h][:])
-            nc.scalar.activation(sig[:, cols], z_acc[h][:], ACT.Sigmoid)
-        shrink = math.exp(-0.3)
-        for cols in halves:
+            nc.scalar.activation(sig[:, cols], neg_z_acc[h][:], ACT.Sigmoid)
+        shrink = math.exp(-SPEED_FLOOR)
+        for cols in cell_halves:
             nc.scalar.activation(log_sig[:, cols], sig[:, cols], ACT.Ln, scale=shrink, bias=shrink * TINY)
 
-        ul, ur, nl, nr = f32("ul"), f32("ur"), f32("nl"), f32("nr")
-        nc.vector.tensor_copy(ul[:], y[:].indirect(lc_t[:]))
-        nc.vector.tensor_copy(ur[:], y[:].indirect(rc_t[:]))
-        half_sq = f32("half_sq")
+        face_halves = halves_of(U)
+        ul, ur, neg_al, neg_ar = f32("ul", U), f32("ur", U), f32("neg_al", U), f32("neg_ar", U)
+        jump, total = f32("jump", U), f32("total", U)
+        for cols in face_halves:
+            nc.vector.tensor_copy(ul[:, cols], looked_up(y, lc_t, cols))
+            nc.vector.tensor_copy(ur[:, cols], looked_up(y, rc_t, cols))
+            nc.gpsimd.tensor_tensor(jump[:, cols], ur[:, cols], ul[:, cols], ALU.subtract)
+            nc.gpsimd.tensor_tensor(total[:, cols], ur[:, cols], ul[:, cols], ALU.add)
+        half_sq = f32("half_sq", U)
         nc.scalar.activation(half_sq[:], ul[:], ACT.Square, scale=math.sqrt(0.5))
-        jump, total = f32("jump"), f32("total")
-        for h, cols in enumerate(halves):
-            nc.vector.scalar_tensor_tensor(snd[:, cols], z_acc[h][:], -0.3, log_sig[:, cols], ALU.add, ALU.min)
-        nc.gpsimd.tensor_tensor(jump[:], ur[:], ul[:], ALU.subtract)
-        nc.gpsimd.tensor_tensor(total[:], ur[:], ul[:], ALU.add)
-        nc.vector.tensor_copy(nl[:], snd[:].indirect(lc_t[:]))
-        nc.vector.tensor_copy(nr[:], snd[:].indirect(rc_t[:]))
+        for h, cols in enumerate(cell_halves):
+            nc.vector.scalar_tensor_tensor(
+                neg_snd[:, cols], neg_z_acc[h][:], -SPEED_FLOOR, log_sig[:, cols], ALU.add, ALU.min
+            )
+        fwd_l = f32("fwd_l", U)
+        for cols in face_halves:
+            nc.vector.tensor_copy(neg_al[:, cols], looked_up(neg_snd, lc_t, cols))
+            nc.gpsimd.tensor_tensor(fwd_l[:, cols], ul[:, cols], neg_al[:, cols], ALU.subtract)
+        for cols in face_halves:
+            nc.vector.tensor_copy(neg_ar[:, cols], looked_up(neg_snd, rc_t, cols))
 
-        back_l, back_r, fwd_l, fwd_r = f32("back_l"), f32("back_r"), f32("fwd_l"), f32("fwd_r")
-        cap_l, cap_r, sl, sr = f32("cap_l"), f32("cap_r"), f32("sl"), f32("sr")
-        nc.vector.tensor_tensor(back_l[:], ul[:], nl[:], ALU.add)
-        for engine, cols in zip((nc.gpsimd, nc.vector), halves):
-            engine.tensor_tensor(fwd_l[:, cols], ul[:, cols], nl[:, cols], ALU.subtract)
-        nc.vector.tensor_tensor(fwd_r[:], ur[:], nr[:], ALU.subtract)
-        nc.vector.scalar_tensor_tensor(cap_l[:], nl[:], 0.01, back_l[:], ALU.mult, ALU.min)
-        nc.vector.tensor_tensor(back_r[:], ur[:], nr[:], ALU.add)
-        nc.vector.scalar_tensor_tensor(cap_r[:], nr[:], -0.01, fwd_r[:], ALU.mult, ALU.max)
+        back_l, back_r, fwd_r = f32("back_l", U), f32("back_r", U), f32("fwd_r", U)
+        cap_l, cap_r = f32("cap_l", U), f32("cap_r", U)
+        sl, sr = f32("sl", U), f32("sr", U)
+        nc.vector.tensor_tensor(back_l[:], ul[:], neg_al[:], ALU.add)
+        nc.vector.tensor_tensor(fwd_r[:], ur[:], neg_ar[:], ALU.subtract)
+        nc.vector.scalar_tensor_tensor(cap_l[:], neg_al[:], CLAMP, back_l[:], ALU.mult, ALU.min)
+        nc.vector.tensor_tensor(back_r[:], ur[:], neg_ar[:], ALU.add)
+        nc.vector.scalar_tensor_tensor(cap_r[:], neg_ar[:], -CLAMP, fwd_r[:], ALU.mult, ALU.max)
         nc.vector.tensor_tensor(sl[:], cap_l[:], back_r[:], ALU.min)
-        for cols in halves:
+        for cols in face_halves:
             nc.vector.tensor_tensor(sr[:, cols], cap_r[:, cols], fwd_l[:, cols], ALU.max)
 
-        jump_sl, width, root, inv = f32("jump_sl"), f32("width"), f32("root"), f32("inv")
-        lead, numer, corr, flux = f32("lead"), f32("numer"), f32("corr"), f32("flux")
-        for cols in halves:
+        width, root, inv = f32("width", U), f32("root", U), f32("inv", U)
+        jump_sl, lead = f32("jump_sl", U), f32("lead", U)
+        numer, corr, flux = f32("numer", U), f32("corr", U), f32("flux", U)
+        for cols in face_halves:
             nc.vector.tensor_tensor(width[:, cols], sr[:, cols], sl[:, cols], ALU.subtract)
-        for cols in halves:
+        for cols in face_halves:
             nc.scalar.activation(root[:, cols], width[:, cols], ACT.Abs_reciprocal_sqrt)
-        for cols in halves:
+        for cols in face_halves:
             nc.scalar.activation(inv[:, cols], root[:, cols], ACT.Square)
         nc.vector.tensor_tensor(jump_sl[:], jump[:], sl[:], ALU.mult)
-        nc.vector.scalar_tensor_tensor(lead[:], total[:], -0.5, sr[:], ALU.mult, ALU.add)
-        for cols in halves:
+        for cols in face_halves:
+            nc.vector.scalar_tensor_tensor(lead[:, cols], total[:, cols], -0.5, sr[:, cols], ALU.mult, ALU.add)
+        for cols in face_halves:
             nc.vector.tensor_tensor(numer[:, cols], lead[:, cols], jump_sl[:, cols], ALU.mult)
-        for cols in halves:
+        for cols in face_halves:
             nc.vector.tensor_tensor(corr[:, cols], numer[:, cols], inv[:, cols], ALU.mult)
-        for cols in halves:
+        for cols in face_halves:
             nc.vector.tensor_tensor(flux[:, cols], corr[:, cols], half_sq[:, cols], ALU.add)
 
         gain, loss, part, new = f32("gain", V), f32("loss", V), f32("part", V), f32("new", V)
-        cells = [slice(h * V // 2, (h + 1) * V // 2) for h in range(2)]
+        out_halves = halves_of(V)
 
         def outflow(cols):
-            entries = outf_t[:, cols.start // LIST_ROWS : cols.stop // LIST_ROWS]
-            nc.vector.tensor_tensor(loss[:, cols], flux[:].indirect(entries), dt_t[:, cols], ALU.mult)
+            nc.vector.tensor_tensor(loss[:, cols], looked_up(flux, outf_t, cols), dt_t[:, cols], ALU.mult)
 
         nc.vector.tensor_tensor(gain[:], flux[:].indirect(inf_t[:]), dt_t[:], ALU.mult)
-        outflow(cells[0])
+        outflow(out_halves[0])
         nc.vector.tensor_tensor(part[:], gain[:], state_t[:], ALU.add)
-        outflow(cells[1])
-        for cols in cells:
+        outflow(out_halves[1])
+        for cols in out_halves:
             nc.vector.tensor_tensor(new[:, cols], part[:, cols], loss[:, cols], ALU.subtract)
             nc.sync.dma_start(out[:, cols], new[:, cols])

import math
from contextlib import ExitStack

import concourse.mybir as mybir

K, T, S, N, U, V = 1024, 2048, 512, 128, 512, 256
FLOPS = 2 * 2 * K * N * S

F32 = mybir.dt.float32
BF16 = mybir.dt.bfloat16
I32 = mybir.dt.int32
U32 = mybir.dt.uint32
U16 = mybir.dt.uint16
U8 = mybir.dt.uint8
FP8X4 = mybir.dt.float8_e4m3fn_x4
ACT = mybir.ActivationFunctionType
ALU = mybir.AluOpType

P = 128
PACK = 4
PASSES = K // (P * PACK)
QUADRANT = 32
SCALE_ROWS = 4
LIST_ROWS = 16
MX_ALIGN = 64
SPEED_FLOOR = 0.3
CLAMP = 0.01
TINY = 2.0**-63


def halves_of(width):
    return [slice(0, width // 2), slice(width // 2, width)]


def tile_picked_yhllf_step_p_kernel(
    tc, x_words, x_scales, w1, w2, state, dtv, offs, lc, rc, outf, inf, out
):
    nc = tc.nc
    with ExitStack() as ctx:
        lists = ctx.enter_context(tc.tile_pool(name="lists", bufs=1))
        sb = ctx.enter_context(tc.tile_pool(name="sb", bufs=1))
        psum = ctx.enter_context(tc.psum_pool(name="psum", bufs=1))

        def f32(name, width):
            return sb.tile([P, width], F32, name=name)

        def looked_up(window, offsets, cols):
            return window[:].indirect(offsets[:, cols.start // LIST_ROWS : cols.stop // LIST_ROWS])

        def load_list(name, src):
            offsets = lists.tile(list(src.shape), U16, name=name)
            nc.sync.dma_start(offsets[:], src)
            return offsets

        table_scales = sb.tile([P, T], U8, name="table_scales")
        nc.vector.memset(table_scales[:].bitcast(I32), 0)
        for q in range(P // QUADRANT):
            nc.scalar.dma_start(
                table_scales[QUADRANT * q : QUADRANT * q + SCALE_ROWS * PASSES, :].bitcast(I32),
                x_scales[:, SCALE_ROWS * q : SCALE_ROWS * (q + 1), :].bitcast(I32),
            )

        w_raw = []
        for name, w in (("w1_raw", w1), ("w2_raw", w2)):
            raw = sb.tile([P, PASSES, PACK, N], F32, name=name)
            nc.sync.dma_start(raw[:], w.rearrange("(g p t) m -> p g t m", g=PASSES, t=PACK))
            w_raw.append(raw)
        offs_t = load_list("offs_t", offs)
        table_words = []
        for g in range(PASSES):
            words = sb.tile([P, T], U32, name="table_words%d" % g)
            nc.sync.dma_start(words[:].bitcast(I32), x_words[g].rearrange("p c t -> p (c t)").bitcast(I32))
            table_words.append(words)
        lc_t = load_list("lc_t", lc)
        rc_t = load_list("rc_t", rc)
        outf_t = load_list("outf_t", outf)
        inf_t = load_list("inf_t", inf)
        state_t = f32("state_t", V)
        dt_t = f32("dt_t", V)
        nc.sync.dma_start(state_t[:], state)
        nc.sync.dma_start(dt_t[:], dtv)

        warm_in, warm_out = f32("warm_in", 8), f32("warm_out", 8)
        nc.vector.memset(warm_in[:], 0.0)
        nc.scalar.activation(warm_out[:], warm_in[:], ACT.Sigmoid)

        w_codes, w_scales = [], []
        for i, (raw, sign) in enumerate(zip(w_raw, (1.0, -1.0))):
            grouped = sb.tile([P, PASSES, N, PACK], BF16, name="grouped", tag="grouped%d" % i, align_bytes=MX_ALIGN)
            nc.vector.tensor_scalar(grouped[:], raw[:].rearrange("p g t m -> p g m t"), sign, None, ALU.mult)
            codes = sb.tile([P, PASSES * N], U32, name="w_codes%d" % i, align_bytes=MX_ALIGN)
            scales = sb.tile([P, PASSES * N], U8, name="w_scales%d" % i, align_bytes=MX_ALIGN)
            nc.vector.quantize_mx(
                out=codes[:].bitcast(FP8X4), scales=scales[:], in_=grouped[:].rearrange("p g m t -> p (g m t)")
            )
            w_codes.append(codes)
            w_scales.append(scales)

        picked_scales = sb.tile([P, S], U8, name="picked_scales", tag="grouped1", align_bytes=MX_ALIGN)
        nc.vector.tensor_copy(picked_scales[:], table_scales[:].indirect(offs_t[:]))

        cell_halves = halves_of(S)
        acc = [[psum.tile([P, S // 2], F32, name="acc%d%d" % (i, h)) for h in range(2)] for i in range(2)]
        for g in range(PASSES):
            for h, cols in enumerate(cell_halves):
                picked = sb.tile([P, S // 2], U32, name="picked%d%d" % (g, h), align_bytes=MX_ALIGN)
                nc.vector.tensor_copy(picked[:], looked_up(table_words[g], offs_t, cols))
                for i in range(2):
                    nc.tensor.matmul_mx(
                        out=acc[i][h][:],
                        lhsT=w_codes[i][:, g * N : (g + 1) * N].bitcast(FP8X4),
                        lhsT_scale=w_scales[i][:, g * N : (g + 1) * N],
                        rhs=picked[:].bitcast(FP8X4),
                        rhs_scale=picked_scales[SCALE_ROWS * g :, cols],
                        start=(g == 0),
                        stop=(g == PASSES - 1),
                    )
        y_acc, neg_z_acc = acc

        y, neg_snd = f32("y", S), f32("neg_snd", S)
        sig, log_sig = f32("sig", S), f32("log_sig", S)
        for h, cols in enumerate(cell_halves):
            nc.scalar.copy(y[:, cols], y_acc[h][:])
            nc.scalar.activation(sig[:, cols], neg_z_acc[h][:], ACT.Sigmoid)
        shrink = math.exp(-SPEED_FLOOR)
        for cols in cell_halves:
            nc.scalar.activation(log_sig[:, cols], sig[:, cols], ACT.Ln, scale=shrink, bias=shrink * TINY)

        face_halves = halves_of(U)
        ul, ur, neg_al, neg_ar = f32("ul", U), f32("ur", U), f32("neg_al", U), f32("neg_ar", U)
        jump, total = f32("jump", U), f32("total", U)
        for cols in face_halves:
            nc.vector.tensor_copy(ul[:, cols], looked_up(y, lc_t, cols))
            nc.vector.tensor_copy(ur[:, cols], looked_up(y, rc_t, cols))
            nc.gpsimd.tensor_tensor(jump[:, cols], ur[:, cols], ul[:, cols], ALU.subtract)
            nc.gpsimd.tensor_tensor(total[:, cols], ur[:, cols], ul[:, cols], ALU.add)
        half_sq = f32("half_sq", U)
        nc.scalar.activation(half_sq[:], ul[:], ACT.Square, scale=math.sqrt(0.5))
        for h, cols in enumerate(cell_halves):
            nc.vector.scalar_tensor_tensor(
                neg_snd[:, cols], neg_z_acc[h][:], -SPEED_FLOOR, log_sig[:, cols], ALU.add, ALU.min
            )
        fwd_l = f32("fwd_l", U)
        for cols in face_halves:
            nc.vector.tensor_copy(neg_al[:, cols], looked_up(neg_snd, lc_t, cols))
            nc.gpsimd.tensor_tensor(fwd_l[:, cols], ul[:, cols], neg_al[:, cols], ALU.subtract)
        for cols in face_halves:
            nc.vector.tensor_copy(neg_ar[:, cols], looked_up(neg_snd, rc_t, cols))

        back_l, back_r, fwd_r = f32("back_l", U), f32("back_r", U), f32("fwd_r", U)
        cap_l, cap_r = f32("cap_l", U), f32("cap_r", U)
        sl, sr = f32("sl", U), f32("sr", U)
        nc.vector.tensor_tensor(back_l[:], ul[:], neg_al[:], ALU.add)
        nc.vector.tensor_tensor(fwd_r[:], ur[:], neg_ar[:], ALU.subtract)
        nc.vector.scalar_tensor_tensor(cap_l[:], neg_al[:], CLAMP, back_l[:], ALU.mult, ALU.min)
        nc.vector.tensor_tensor(back_r[:], ur[:], neg_ar[:], ALU.add)
        nc.vector.scalar_tensor_tensor(cap_r[:], neg_ar[:], -CLAMP, fwd_r[:], ALU.mult, ALU.max)
        nc.vector.tensor_tensor(sl[:], cap_l[:], back_r[:], ALU.min)
        for cols in face_halves:
            nc.vector.tensor_tensor(sr[:, cols], cap_r[:, cols], fwd_l[:, cols], ALU.max)

        width, root, inv = f32("width", U), f32("root", U), f32("inv", U)
        jump_sl, lead = f32("jump_sl", U), f32("lead", U)
        numer, corr, flux = f32("numer", U), f32("corr", U), f32("flux", U)
        for cols in face_halves:
            nc.vector.tensor_tensor(width[:, cols], sr[:, cols], sl[:, cols], ALU.subtract)
        for cols in face_halves:
            nc.scalar.activation(root[:, cols], width[:, cols], ACT.Abs_reciprocal_sqrt)
        for cols in face_halves:
            nc.scalar.activation(inv[:, cols], root[:, cols], ACT.Square)
        nc.vector.tensor_tensor(jump_sl[:], jump[:], sl[:], ALU.mult)
        for cols in face_halves:
            nc.vector.scalar_tensor_tensor(lead[:, cols], total[:, cols], -0.5, sr[:, cols], ALU.mult, ALU.add)
        for cols in face_halves:
            nc.vector.tensor_tensor(numer[:, cols], lead[:, cols], jump_sl[:, cols], ALU.mult)
        for cols in face_halves:
            nc.vector.tensor_tensor(corr[:, cols], numer[:, cols], inv[:, cols], ALU.mult)
        for cols in face_halves:
            nc.vector.tensor_tensor(flux[:, cols], corr[:, cols], half_sq[:, cols], ALU.add)

        gain, loss, part, new = f32("gain", V), f32("loss", V), f32("part", V), f32("new", V)
        out_halves = halves_of(V)

        def outflow(cols):
            nc.vector.tensor_tensor(loss[:, cols], looked_up(flux, outf_t, cols), dt_t[:, cols], ALU.mult)

        nc.vector.tensor_tensor(gain[:], flux[:].indirect(inf_t[:]), dt_t[:], ALU.mult)
        outflow(out_halves[0])
        nc.vector.tensor_tensor(part[:], gain[:], state_t[:], ALU.add)
        outflow(out_halves[1])
        for cols in out_halves:
            nc.vector.tensor_tensor(new[:, cols], part[:, cols], loss[:, cols], ALU.subtract)
            nc.sync.dma_start(out[:, cols], new[:, cols])
